import numpy as np
import ml_dtypes


def mxq(x, axis, fmt="e4m3"):
    dtype, down = {"e4m3": (ml_dtypes.float8_e4m3fn, 7), "e5m2": (ml_dtypes.float8_e5m2, 14)}[fmt]
    v = np.moveaxis(np.asarray(x, np.float32).astype(ml_dtypes.bfloat16).astype(np.float64), axis, -1)
    blocks = v.reshape(v.shape[:-1] + (-1, 32))
    amax = np.abs(blocks).max(-1, keepdims=True)
    byte = np.maximum(np.where(amax > 0, np.frexp(amax)[1] - 1 + 127, 0) - down, 1)
    scale = np.exp2(byte - 127.0)
    codes = (blocks / scale).astype(np.float32).astype(dtype).astype(np.float64)
    return np.moveaxis((codes * scale).reshape(v.shape), -1, axis)


WIDE = False


def mx_kscale(k, group=512):
    if not WIDE:
        return np.ones(k)
    levels = np.array([10, -10, 5, -5, 0])
    if group != 512:
        return np.exp2(np.random.permutation(np.resize(levels, k // group))).repeat(group)
    if k % 512:
        return np.exp2(np.random.permutation(np.resize(levels, k // 32))).repeat(32)
    a = np.empty((k // 512, 16))
    for p in range(k // 512):
        a[p, :8] = np.random.permutation(np.resize(levels, 8))
        for g in range(8):
            far = levels[np.abs(levels - a[p, g]) >= 10]
            a[p, g + 8] = far[np.random.randint(len(far))]
    return np.exp2(a.ravel()).repeat(32)


def f64(x):
    return np.asarray(x).astype(np.float64)


G, D, M, N = 4, 256, 128, 1024


def setup_inputs():
    n = np.random.standard_normal
    s = mx_kscale(D, 0)[:, None]
    return {
        "x": (n((G, D, N)) * s).astype(np.float32),
        "w": (n((G, D, M)) / np.sqrt(D) / s).astype(np.float32),
        "u": (n((G, D, M)) / np.sqrt(D) / s).astype(np.float32),
        "r": n((G, M, N)).astype(np.float32),
    }


def reference(x, w, u, r):
    xq = mxq(f64(x), 1, "e4m3")
    h = mxq(f64(w), 1, "e4m3").transpose(0, 2, 1) @ xq
    g = mxq(f64(u), 1, "e4m3").transpose(0, 2, 1) @ xq
    y = np.maximum(h, 0.0) * g
    y = y + f64(r)
    return y

@@ -1,0 +1,181 @@
+from contextlib import ExitStack
+
+import concourse.mybir as mybir
+
+G, D, M, N = 4, 256, 128, 1024
+FLOPS = 2 * 2 * G * D * M * N
+
+F32 = mybir.dt.float32
+BF16 = mybir.dt.bfloat16
+U32 = mybir.dt.uint32
+U8 = mybir.dt.uint8
+FP8X4 = mybir.dt.float8_e4m3fn_x4
+ALU = mybir.AluOpType
+
+P = 128
+PACK = 4
+ROWS = D // PACK
+SIDE = P // ROWS
+PAIRS = G // SIDE
+CHUNK = 512
+HALVES = N // CHUNK
+RUN = 4
+VECTOR_COLS = 320
+
+
+def interleave(copy, dst, src):
+    copy(
+        out=dst.rearrange("p (c i) j -> p c j i", i=RUN),
+        in_=src.rearrange("p j (c i) -> p c j i", i=RUN),
+    )
+
+
+def tile_rows_gglu_relu_res_kernel(tc, x, w, u, r, out):
+    nc = tc.nc
+    x_rows = x.rearrange("(s c) (p j) n -> s (c p) j n", c=SIDE, j=PACK)
+    w_rows = w.rearrange("(s c) (p j) m -> s (c p) j m", c=SIDE, j=PACK)
+    u_rows = u.rearrange("(s c) (p j) m -> s (c p) j m", c=SIDE, j=PACK)
+
+    with ExitStack() as ctx:
+        sb = ctx.enter_context(tc.tile_pool(name="sb", bufs=1))
+        psum = ctx.enter_context(tc.psum_pool(name="psum", bufs=1))
+        ctx.enter_context(tc.manual_schedule())
+
+        chunks = [(s, h) for s in range(PAIRS) for h in range(HALVES)]
+        x_raw = {k: sb.tile([P, PACK, CHUNK], F32, name="x_raw_%d_%d" % k) for k in chunks}
+        x_bf = {k: sb.tile([P, CHUNK, PACK], BF16, name="x_bf_%d_%d" % k, align_bytes=64) for k in chunks}
+        x_codes = {k: sb.tile([P, CHUNK], U32, name="x_codes_%d_%d" % k, align_bytes=64) for k in chunks}
+        x_scales = {k: sb.tile([P, CHUNK], U8, name="x_scales_%d_%d" % k, align_bytes=64) for k in chunks}
+        w_raw = [sb.tile([P, PACK, M], F32, name="w_raw_%d" % s) for s in range(PAIRS)]
+        u_raw = [sb.tile([P, PACK, M], F32, name="u_raw_%d" % s) for s in range(PAIRS)]
+        wu_bf = [sb.tile([P, 2 * M, PACK], BF16, name="wu_bf_%d" % s, align_bytes=64) for s in range(PAIRS)]
+        wu_codes = [sb.tile([P, 2 * M], U32, name="wu_codes_%d" % s, align_bytes=64) for s in range(PAIRS)]
+        wu_scales = [sb.tile([P, 2 * M], U8, name="wu_scales_%d" % s, align_bytes=64) for s in range(PAIRS)]
+        r_sb = [sb.tile([M, N], F32, name="r_sb_%d" % g) for g in range(G)]
+        gate_sb = [sb.tile([M, N], F32, name="gate_sb_%d" % g) for g in range(G)]
+        prod = [sb.tile([M, N], F32, name="prod_%d" % g) for g in range(G)]
+        y = [sb.tile([M, N], F32, name="y_%d" % g) for g in range(G)]
+        z_ps = {(c, h): psum.tile([M, CHUNK], F32, name="z_ps_%d_%d" % (c, h)) for c in range(SIDE) for h in range(HALVES)}
+        gate_ps = {(c, h): psum.tile([M, CHUNK], F32, name="gate_ps_%d_%d" % (c, h)) for c in range(SIDE) for h in range(HALVES)}
+
+        def cols(h):
+            return slice(h * CHUNK, (h + 1) * CHUNK)
+
+        def load_weights(s):
+            nc.sync.dma_start(out=w_raw[s][:], in_=w_rows[s])
+            nc.sync.dma_start(out=u_raw[s][:], in_=u_rows[s])
+
+        def load_x(s, h):
+            nc.sync.dma_start(out=x_raw[s, h][:], in_=x_rows[s][:, :, cols(h)])
+
+        def load_r(g):
+            nc.sync.dma_start(out=r_sb[g][:], in_=r[g])
+
+        def round_weights(s):
+            interleave(nc.scalar.copy, wu_bf[s][:, 0:M, :], w_raw[s][:])
+            interleave(nc.vector.tensor_copy, wu_bf[s][:, M : 2 * M, :], u_raw[s][:])
+
+        def quantize_weights(s):
+            nc.vector.quantize_mx(
+                out=wu_codes[s][:].bitcast(FP8X4),
+                scales=wu_scales[s][:],
+                in_=wu_bf[s][:].rearrange("p m j -> p (m j)"),
+            )
+
+        def round_x(s, h):
+            interleave(nc.vector.tensor_copy, x_bf[s, h][:, 0:VECTOR_COLS, :], x_raw[s, h][:, :, 0:VECTOR_COLS])
+            interleave(nc.scalar.copy, x_bf[s, h][:, VECTOR_COLS:CHUNK, :], x_raw[s, h][:, :, VECTOR_COLS:CHUNK])
+
+        def quantize_x(s, h):
+            nc.vector.quantize_mx(
+                out=x_codes[s, h][:].bitcast(FP8X4),
+                scales=x_scales[s, h][:],
+                in_=x_bf[s, h][:].rearrange("p n j -> p (n j)"),
+            )
+
+        def multiply(s, h):
+            for banks, m_cols in ((gate_ps, slice(M, 2 * M)), (z_ps, slice(0, M))):
+                for c in range(SIDE):
+                    rows = slice(c * ROWS, (c + 1) * ROWS)
+                    nc.tensor.matmul_mx(
+                        out=banks[c, h][:],
+                        lhsT=wu_codes[s][rows, m_cols].bitcast(FP8X4),
+                        lhsT_scale=wu_scales[s][rows, m_cols],
+                        rhs=x_codes[s, h][rows, :].bitcast(FP8X4),
+                        rhs_scale=x_scales[s, h][rows, :],
+                        start=True,
+                        stop=True,
+                    )
+
+        def copy_gates(s, h):
+            for c in range(SIDE):
+                nc.scalar.copy(out=gate_sb[SIDE * s + c][:, cols(h)], in_=gate_ps[c, h][:])
+
+        def gate(s, h):
+            for c in range(SIDE):
+                g = SIDE * s + c
+                nc.vector.scalar_tensor_tensor(
+                    out=prod[g][:, cols(h)],
+                    in0=z_ps[c, h][:],
+                    scalar=0.0,
+                    in1=gate_sb[g][:, cols(h)],
+                    op0=ALU.max,
+                    op1=ALU.mult,
+                )
+
+        def add_residual(g, span):
+            nc.vector.tensor_tensor(out=y[g][:, span], in0=prod[g][:, span], in1=r_sb[g][:, span], op=ALU.add)
+
+        def store(g, span):
+            nc.sync.dma_start(out=out[g][:, span], in_=y[g][:, span])
+
+        whole = slice(0, N)
+
+        load_weights(0)
+        load_x(0, 0)
+        load_x(0, 1)
+        load_weights(1)
+        load_r(0)
+        load_x(1, 0)
+        load_r(1)
+        load_x(1, 1)
+        load_r(2)
+        load_r(3)
+
+        round_weights(0)
+        quantize_weights(0)
+        round_x(0, 0)
+        quantize_x(0, 0)
+        multiply(0, 0)
+        round_x(0, 1)
+        copy_gates(0, 0)
+        quantize_x(0, 1)
+        multiply(0, 1)
+        gate(0, 0)
+        round_weights(1)
+        copy_gates(0, 1)
+        quantize_weights(1)
+        gate(0, 1)
+        add_residual(0, whole)
+        round_x(1, 0)
+        quantize_x(1, 0)
+        multiply(1, 0)
+        add_residual(1, whole)
+        copy_gates(1, 0)
+        gate(1, 0)
+        round_x(1, 1)
+        quantize_x(1, 1)
+        multiply(1, 1)
+        add_residual(2, cols(0))
+        add_residual(3, cols(0))
+        copy_gates(1, 1)
+        gate(1, 1)
+        add_residual(2, cols(1))
+        add_residual(3, cols(1))
+
+        store(0, whole)
+        store(1, whole)
+        store(2, cols(0))
+        store(3, cols(0))
+        store(2, cols(1))
+        store(3, cols(1))

@@ -36,44 +36,49 @@ def tile_rows_gglu_relu_res_kernel(tc, x, w, u, r, out):
     w_rows = w.rearrange("(s c) (p j) m -> s (c p) j m", c=SIDE, j=PACK)
     u_rows = u.rearrange("(s c) (p j) m -> s (c p) j m", c=SIDE, j=PACK)
 
+    r_rows = r.rearrange("(s c) m n -> s m c n", c=SIDE)
+
     with ExitStack() as ctx:
         sb = ctx.enter_context(tc.tile_pool(name="sb", bufs=1))
         psum = ctx.enter_context(tc.psum_pool(name="psum", bufs=1))
         ctx.enter_context(tc.manual_schedule())
 
         chunks = [(s, h) for s in range(PAIRS) for h in range(HALVES)]
-        x_raw = {k: sb.tile([P, PACK, CHUNK], F32, name="x_raw_%d_%d" % k) for k in chunks}
-        x_bf = {k: sb.tile([P, CHUNK, PACK], BF16, name="x_bf_%d_%d" % k, align_bytes=64) for k in chunks}
-        x_codes = {k: sb.tile([P, CHUNK], U32, name="x_codes_%d_%d" % k, align_bytes=64) for k in chunks}
-        x_scales = {k: sb.tile([P, CHUNK], U8, name="x_scales_%d_%d" % k, align_bytes=64) for k in chunks}
+        steps = range(len(chunks))
+        places = range(SIDE)
+        x_raw = [sb.tile([P, PACK, CHUNK], F32, name="x_raw_%d" % i) for i in steps]
+        x_bf = [sb.tile([P, CHUNK, PACK], BF16, name="x_bf_%d" % i, align_bytes=64) for i in steps]
+        x_codes = [sb.tile([P, CHUNK], U32, name="x_codes_%d" % i, align_bytes=64) for i in steps]
+        x_scales = [sb.tile([P, CHUNK], U8, name="x_scales_%d" % i, align_bytes=64) for i in steps]
         w_raw = [sb.tile([P, PACK, M], F32, name="w_raw_%d" % s) for s in range(PAIRS)]
         u_raw = [sb.tile([P, PACK, M], F32, name="u_raw_%d" % s) for s in range(PAIRS)]
         wu_bf = [sb.tile([P, 2 * M, PACK], BF16, name="wu_bf_%d" % s, align_bytes=64) for s in range(PAIRS)]
         wu_codes = [sb.tile([P, 2 * M], U32, name="wu_codes_%d" % s, align_bytes=64) for s in range(PAIRS)]
         wu_scales = [sb.tile([P, 2 * M], U8, name="wu_scales_%d" % s, align_bytes=64) for s in range(PAIRS)]
-        r_sb = [sb.tile([M, N], F32, name="r_sb_%d" % g) for g in range(G)]
-        gate_sb = [sb.tile([M, N], F32, name="gate_sb_%d" % g) for g in range(G)]
-        prod = [sb.tile([M, N], F32, name="prod_%d" % g) for g in range(G)]
-        y = [sb.tile([M, N], F32, name="y_%d" % g) for g in range(G)]
-        z_ps = {(c, h): psum.tile([M, CHUNK], F32, name="z_ps_%d_%d" % (c, h)) for c in range(SIDE) for h in range(HALVES)}
-        gate_ps = {(c, h): psum.tile([M, CHUNK], F32, name="gate_ps_%d_%d" % (c, h)) for c in range(SIDE) for h in range(HALVES)}
+        r_sb = [sb.tile([M, SIDE, CHUNK], F32, name="r_sb_%d" % i) for i in steps]
+        gate_sb = {(i, c): sb.tile([M, CHUNK], F32, name="gate_sb_%d_%d" % (i, c)) for i in steps for c in places}
+        prod = {(i, c): sb.tile([M, CHUNK], F32, name="prod_%d_%d" % (i, c)) for i in steps for c in places}
+        y = {(i, c): sb.tile([M, CHUNK], F32, name="y_%d_%d" % (i, c)) for i in steps for c in places}
+        z_ps = {(h, c): psum.tile([M, CHUNK], F32, name="z_ps_%d_%d" % (h, c)) for h in range(HALVES) for c in places}
+        gate_ps = {(h, c): psum.tile([M, CHUNK], F32, name="gate_ps_%d_%d" % (h, c)) for h in range(HALVES) for c in places}
 
-        def cols(h):
+        def cols(i):
+            h = chunks[i][1]
             return slice(h * CHUNK, (h + 1) * CHUNK)
 
         def load_weights(s):
             nc.sync.dma_start(out=w_raw[s][:], in_=w_rows[s])
             nc.sync.dma_start(out=u_raw[s][:], in_=u_rows[s])
 
-        def load_x(s, h):
-            nc.sync.dma_start(out=x_raw[s, h][:], in_=x_rows[s][:, :, cols(h)])
+        def load_x(i):
+            nc.sync.dma_start(out=x_raw[i][:], in_=x_rows[chunks[i][0]][:, :, cols(i)])
 
-        def load_r(g):
-            nc.sync.dma_start(out=r_sb[g][:], in_=r[g])
+        def load_r(i):
+            nc.sync.dma_start(out=r_sb[i][:], in_=r_rows[chunks[i][0]][:, :, cols(i)])
 
         def round_weights(s):
             interleave(nc.scalar.copy, wu_bf[s][:, 0:M, :], w_raw[s][:])
-            interleave(nc.vector.tensor_copy, wu_bf[s][:, M : 2 * M, :], u_raw[s][:])
+            interleave(nc.scalar.copy, wu_bf[s][:, M : 2 * M, :], u_raw[s][:])
 
         def quantize_weights(s):
             nc.vector.quantize_mx(
@@ -82,100 +87,83 @@ def tile_rows_gglu_relu_res_kernel(tc, x, w, u, r, out):
                 in_=wu_bf[s][:].rearrange("p m j -> p (m j)"),
             )
 
-        def round_x(s, h):
-            interleave(nc.vector.tensor_copy, x_bf[s, h][:, 0:VECTOR_COLS, :], x_raw[s, h][:, :, 0:VECTOR_COLS])
-            interleave(nc.scalar.copy, x_bf[s, h][:, VECTOR_COLS:CHUNK, :], x_raw[s, h][:, :, VECTOR_COLS:CHUNK])
+        def round_x(i):
+            interleave(nc.vector.tensor_copy, x_bf[i][:, 0:VECTOR_COLS, :], x_raw[i][:, :, 0:VECTOR_COLS])
+            interleave(nc.scalar.copy, x_bf[i][:, VECTOR_COLS:CHUNK, :], x_raw[i][:, :, VECTOR_COLS:CHUNK])
 
-        def quantize_x(s, h):
+        def quantize_x(i):
             nc.vector.quantize_mx(
-                out=x_codes[s, h][:].bitcast(FP8X4),
-                scales=x_scales[s, h][:],
-                in_=x_bf[s, h][:].rearrange("p n j -> p (n j)"),
+                out=x_codes[i][:].bitcast(FP8X4),
+                scales=x_scales[i][:],
+                in_=x_bf[i][:].rearrange("p n j -> p (n j)"),
             )
 
-        def multiply(s, h):
+        def multiply(i):
+            s, h = chunks[i]
             for banks, m_cols in ((gate_ps, slice(M, 2 * M)), (z_ps, slice(0, M))):
-                for c in range(SIDE):
+                for c in places:
                     rows = slice(c * ROWS, (c + 1) * ROWS)
                     nc.tensor.matmul_mx(
-                        out=banks[c, h][:],
+                        out=banks[h, c][:],
                         lhsT=wu_codes[s][rows, m_cols].bitcast(FP8X4),
                         lhsT_scale=wu_scales[s][rows, m_cols],
-                        rhs=x_codes[s, h][rows, :].bitcast(FP8X4),
-                        rhs_scale=x_scales[s, h][rows, :],
+                        rhs=x_codes[i][rows, :].bitcast(FP8X4),
+                        rhs_scale=x_scales[i][rows, :],
                         start=True,
                         stop=True,
                     )
 
-        def copy_gates(s, h):
-            for c in range(SIDE):
-                nc.scalar.copy(out=gate_sb[SIDE * s + c][:, cols(h)], in_=gate_ps[c, h][:])
+        def copy_gates(i):
+            for c in places:
+                nc.scalar.copy(out=gate_sb[i, c][:], in_=gate_ps[chunks[i][1], c][:])
 
-        def gate(s, h):
-            for c in range(SIDE):
-                g = SIDE * s + c
+        def apply_gates(i):
+            for c in places:
                 nc.vector.scalar_tensor_tensor(
-                    out=prod[g][:, cols(h)],
-                    in0=z_ps[c, h][:],
+                    out=prod[i, c][:],
+                    in0=z_ps[chunks[i][1], c][:],
                     scalar=0.0,
-                    in1=gate_sb[g][:, cols(h)],
+                    in1=gate_sb[i, c][:],
                     op0=ALU.max,
                     op1=ALU.mult,
                 )
 
-        def add_residual(g, span):
-            nc.vector.tensor_tensor(out=y[g][:, span], in0=prod[g][:, span], in1=r_sb[g][:, span], op=ALU.add)
+        def add_residual(engine, result, i, c):
+            engine.tensor_tensor(out=result[:], in0=prod[i, c][:], in1=r_sb[i][:, c, :], op=ALU.add)
 
-        def store(g, span):
-            nc.sync.dma_start(out=out[g][:, span], in_=y[g][:, span])
-
-        whole = slice(0, N)
+        def store(result, i, c):
+            nc.sync.dma_start(out=out[SIDE * chunks[i][0] + c][:, cols(i)], in_=result[:])
 
         load_weights(0)
-        load_x(0, 0)
-        load_x(0, 1)
+        for i in (0, 1, 2):
+            load_x(i)
         load_weights(1)
         load_r(0)
-        load_x(1, 0)
-        load_r(1)
-        load_x(1, 1)
-        load_r(2)
-        load_r(3)
+        load_x(3)
+        for i in (1, 2, 3):
+            load_r(i)
 
         round_weights(0)
         quantize_weights(0)
-        round_x(0, 0)
-        quantize_x(0, 0)
-        multiply(0, 0)
-        round_x(0, 1)
-        copy_gates(0, 0)
-        quantize_x(0, 1)
-        multiply(0, 1)
-        gate(0, 0)
-        round_weights(1)
-        copy_gates(0, 1)
-        quantize_weights(1)
-        gate(0, 1)
-        add_residual(0, whole)
-        round_x(1, 0)
-        quantize_x(1, 0)
-        multiply(1, 0)
-        add_residual(1, whole)
-        copy_gates(1, 0)
-        gate(1, 0)
-        round_x(1, 1)
-        quantize_x(1, 1)
-        multiply(1, 1)
-        add_residual(2, cols(0))
-        add_residual(3, cols(0))
-        copy_gates(1, 1)
-        gate(1, 1)
-        add_residual(2, cols(1))
-        add_residual(3, cols(1))
-
-        store(0, whole)
-        store(1, whole)
-        store(2, cols(0))
-        store(3, cols(0))
-        store(2, cols(1))
-        store(3, cols(1))
+        last = len(chunks) - 1
+        for i in range(last + 3):
+            if i <= last:
+                round_x(i)
+                quantize_x(i)
+                if i == HALVES:
+                    round_weights(1)
+                    quantize_weights(1)
+                multiply(i)
+            if 0 <= i - 1 <= last:
+                copy_gates(i - 1)
+            if 0 <= i - 2 < last:
+                add_residual(nc.vector, y[i - 2, 1], i - 2, 1)
+                add_residual(nc.gpsimd, prod[i - 2, 1], i - 2, 0)
+                store(y[i - 2, 1], i - 2, 1)
+                store(prod[i - 2, 1], i - 2, 0)
+            if i - 2 == last:
+                for c in places:
+                    add_residual(nc.vector, y[last, c], last, c)
+                    store(y[last, c], last, c)
+            if 0 <= i - 1 <= last:
+                apply_gates(i - 1)

@@ -19,8 +19,10 @@ SIDE = P // ROWS
 PAIRS = G // SIDE
 CHUNK = 512
 HALVES = N // CHUNK
-RUN = 4
+RUN = 2
 VECTOR_COLS = 320
+GPSIMD_COLS = 384
+SPLIT = SIDE * CHUNK - GPSIMD_COLS
 
 
 def interleave(copy, dst, src):
@@ -55,10 +57,9 @@ def tile_rows_gglu_relu_res_kernel(tc, x, w, u, r, out):
         wu_bf = [sb.tile([P, 2 * M, PACK], BF16, name="wu_bf_%d" % s, align_bytes=64) for s in range(PAIRS)]
         wu_codes = [sb.tile([P, 2 * M], U32, name="wu_codes_%d" % s, align_bytes=64) for s in range(PAIRS)]
         wu_scales = [sb.tile([P, 2 * M], U8, name="wu_scales_%d" % s, align_bytes=64) for s in range(PAIRS)]
-        r_sb = [sb.tile([M, SIDE, CHUNK], F32, name="r_sb_%d" % i) for i in steps]
+        r_sb = [sb.tile([M, SIDE * CHUNK], F32, name="r_sb_%d" % i) for i in steps]
         gate_sb = {(i, c): sb.tile([M, CHUNK], F32, name="gate_sb_%d_%d" % (i, c)) for i in steps for c in places}
-        prod = {(i, c): sb.tile([M, CHUNK], F32, name="prod_%d_%d" % (i, c)) for i in steps for c in places}
-        y = {(i, c): sb.tile([M, CHUNK], F32, name="y_%d_%d" % (i, c)) for i in steps for c in places}
+        work = [sb.tile([M, SPLIT + SIDE * CHUNK], F32, name="work_%d" % i) for i in steps]
         z_ps = {(h, c): psum.tile([M, CHUNK], F32, name="z_ps_%d_%d" % (h, c)) for h in range(HALVES) for c in places}
         gate_ps = {(h, c): psum.tile([M, CHUNK], F32, name="gate_ps_%d_%d" % (h, c)) for h in range(HALVES) for c in places}
 
@@ -74,7 +75,7 @@ def tile_rows_gglu_relu_res_kernel(tc, x, w, u, r, out):
             nc.sync.dma_start(out=x_raw[i][:], in_=x_rows[chunks[i][0]][:, :, cols(i)])
 
         def load_r(i):
-            nc.sync.dma_start(out=r_sb[i][:], in_=r_rows[chunks[i][0]][:, :, cols(i)])
+            nc.sync.dma_start(out=r_sb[i][:].rearrange("m (c n) -> m c n", c=SIDE), in_=r_rows[chunks[i][0]][:, :, cols(i)])
 
         def round_weights(s):
             interleave(nc.scalar.copy, wu_bf[s][:, 0:M, :], w_raw[s][:])
@@ -120,7 +121,7 @@ def tile_rows_gglu_relu_res_kernel(tc, x, w, u, r, out):
         def apply_gates(i):
             for c in places:
                 nc.vector.scalar_tensor_tensor(
-                    out=prod[i, c][:],
+                    out=work[i][:, SPLIT + c * CHUNK : SPLIT + (c + 1) * CHUNK],
                     in0=z_ps[chunks[i][1], c][:],
                     scalar=0.0,
                     in1=gate_sb[i, c][:],
@@ -128,11 +129,13 @@ def tile_rows_gglu_relu_res_kernel(tc, x, w, u, r, out):
                     op1=ALU.mult,
                 )
 
-        def add_residual(engine, result, i, c):
-            engine.tensor_tensor(out=result[:], in0=prod[i, c][:], in1=r_sb[i][:, c, :], op=ALU.add)
+        def add_residual(engine, i, lo, hi):
+            engine.tensor_tensor(
+                out=work[i][:, lo:hi], in0=work[i][:, SPLIT + lo : SPLIT + hi], in1=r_sb[i][:, lo:hi], op=ALU.add
+            )
 
-        def store(result, i, c):
-            nc.sync.dma_start(out=out[SIDE * chunks[i][0] + c][:, cols(i)], in_=result[:])
+        def store(i, c):
+            nc.sync.dma_start(out=out[SIDE * chunks[i][0] + c][:, cols(i)], in_=work[i][:, c * CHUNK : (c + 1) * CHUNK])
 
         load_weights(0)
         for i in (0, 1, 2):
@@ -157,13 +160,13 @@ def tile_rows_gglu_relu_res_kernel(tc, x, w, u, r, out):
             if 0 <= i - 1 <= last:
                 copy_gates(i - 1)
             if 0 <= i - 2 < last:
-                add_residual(nc.vector, y[i - 2, 1], i - 2, 1)
-                add_residual(nc.gpsimd, prod[i - 2, 1], i - 2, 0)
-                store(y[i - 2, 1], i - 2, 1)
-                store(prod[i - 2, 1], i - 2, 0)
+                add_residual(nc.vector, i - 2, 0, SPLIT)
+                add_residual(nc.gpsimd, i - 2, SPLIT, SIDE * CHUNK)
+                for c in places:
+                    store(i - 2, c)
             if i - 2 == last:
                 for c in places:
-                    add_residual(nc.vector, y[last, c], last, c)
-                    store(y[last, c], last, c)
+                    add_residual(nc.vector, last, c * CHUNK, (c + 1) * CHUNK)
+                    store(last, c)
             if 0 <= i - 1 <= last:
                 apply_gates(i - 1)

@@ -20,9 +20,8 @@ PAIRS = G // SIDE
 CHUNK = 512
 HALVES = N // CHUNK
 RUN = 2
-VECTOR_COLS = 320
+VECTOR_COLS = (256, 256, 256, 320)
 GPSIMD_COLS = 384
-SPLIT = SIDE * CHUNK - GPSIMD_COLS
 
 
 def interleave(copy, dst, src):
@@ -38,7 +37,6 @@ def tile_rows_gglu_relu_res_kernel(tc, x, w, u, r, out):
     w_rows = w.rearrange("(s c) (p j) m -> s (c p) j m", c=SIDE, j=PACK)
     u_rows = u.rearrange("(s c) (p j) m -> s (c p) j m", c=SIDE, j=PACK)
 
-    r_rows = r.rearrange("(s c) m n -> s m c n", c=SIDE)
 
     with ExitStack() as ctx:
         sb = ctx.enter_context(tc.tile_pool(name="sb", bufs=1))
@@ -48,8 +46,10 @@ def tile_rows_gglu_relu_res_kernel(tc, x, w, u, r, out):
         chunks = [(s, h) for s in range(PAIRS) for h in range(HALVES)]
         steps = range(len(chunks))
         places = range(SIDE)
-        x_raw = [sb.tile([P, PACK, CHUNK], F32, name="x_raw_%d" % i) for i in steps]
-        x_bf = [sb.tile([P, CHUNK, PACK], BF16, name="x_bf_%d" % i, align_bytes=64) for i in steps]
+        x_first = sb.tile([P, PACK, N], F32)
+        x_late = [sb.tile([P, PACK, CHUNK], F32, name="x_late_%d" % h) for h in range(HALVES)]
+        x_raw = [x_first[:, :, 0:CHUNK], x_first[:, :, CHUNK:N], x_late[0][:], x_late[1][:]]
+        x_bf = [sb.tile([P, CHUNK, PACK], BF16, name="x_bf_%d" % i, tag="x_bf_%d" % i, align_bytes=64) for i in steps]
         x_codes = [sb.tile([P, CHUNK], U32, name="x_codes_%d" % i, align_bytes=64) for i in steps]
         x_scales = [sb.tile([P, CHUNK], U8, name="x_scales_%d" % i, align_bytes=64) for i in steps]
         w_raw = [sb.tile([P, PACK, M], F32, name="w_raw_%d" % s) for s in range(PAIRS)]
@@ -57,9 +57,16 @@ def tile_rows_gglu_relu_res_kernel(tc, x, w, u, r, out):
         wu_bf = [sb.tile([P, 2 * M, PACK], BF16, name="wu_bf_%d" % s, align_bytes=64) for s in range(PAIRS)]
         wu_codes = [sb.tile([P, 2 * M], U32, name="wu_codes_%d" % s, align_bytes=64) for s in range(PAIRS)]
         wu_scales = [sb.tile([P, 2 * M], U8, name="wu_scales_%d" % s, align_bytes=64) for s in range(PAIRS)]
-        r_sb = [sb.tile([M, SIDE * CHUNK], F32, name="r_sb_%d" % i) for i in steps]
+        r_sb = [sb.tile([M, N], F32, name="r_sb_%d" % g) for g in range(G)]
         gate_sb = {(i, c): sb.tile([M, CHUNK], F32, name="gate_sb_%d_%d" % (i, c)) for i in steps for c in places}
-        work = [sb.tile([M, SPLIT + SIDE * CHUNK], F32, name="work_%d" % i) for i in steps]
+        prod = [sb.tile([M, N], F32, name="prod_%d" % g) for g in range(G)]
+        y = {g: sb.tile([M, N], F32, name="y_%d" % g) for g in (2, 3)}
+
+        def prod_of(g, lo, hi):
+            if g == 3 and hi <= CHUNK:
+                return y[2][:, lo:hi]
+            return prod[g][:, lo:hi]
+
         z_ps = {(h, c): psum.tile([M, CHUNK], F32, name="z_ps_%d_%d" % (h, c)) for h in range(HALVES) for c in places}
         gate_ps = {(h, c): psum.tile([M, CHUNK], F32, name="gate_ps_%d_%d" % (h, c)) for h in range(HALVES) for c in places}
 
@@ -71,15 +78,15 @@ def tile_rows_gglu_relu_res_kernel(tc, x, w, u, r, out):
             nc.sync.dma_start(out=w_raw[s][:], in_=w_rows[s])
             nc.sync.dma_start(out=u_raw[s][:], in_=u_rows[s])
 
-        def load_x(i):
-            nc.sync.dma_start(out=x_raw[i][:], in_=x_rows[chunks[i][0]][:, :, cols(i)])
+        def load_late_x(h):
+            nc.sync.dma_start(out=x_late[h][:], in_=x_rows[1][:, :, cols(h)])
 
-        def load_r(i):
-            nc.sync.dma_start(out=r_sb[i][:].rearrange("m (c n) -> m c n", c=SIDE), in_=r_rows[chunks[i][0]][:, :, cols(i)])
+        def load_r(g):
+            nc.sync.dma_start(out=r_sb[g][:], in_=r[g])
 
-        def round_weights(s):
-            interleave(nc.scalar.copy, wu_bf[s][:, 0:M, :], w_raw[s][:])
-            interleave(nc.scalar.copy, wu_bf[s][:, M : 2 * M, :], u_raw[s][:])
+        def round_weights(copy, s):
+            interleave(copy, wu_bf[s][:, 0:M, :], w_raw[s][:])
+            interleave(copy, wu_bf[s][:, M : 2 * M, :], u_raw[s][:])
 
         def quantize_weights(s):
             nc.vector.quantize_mx(
@@ -88,9 +95,13 @@ def tile_rows_gglu_relu_res_kernel(tc, x, w, u, r, out):
                 in_=wu_bf[s][:].rearrange("p m j -> p (m j)"),
             )
 
-        def round_x(i):
-            interleave(nc.vector.tensor_copy, x_bf[i][:, 0:VECTOR_COLS, :], x_raw[i][:, :, 0:VECTOR_COLS])
-            interleave(nc.scalar.copy, x_bf[i][:, VECTOR_COLS:CHUNK, :], x_raw[i][:, :, VECTOR_COLS:CHUNK])
+        def round_x_on_vector(i):
+            split = VECTOR_COLS[i]
+            interleave(nc.vector.tensor_copy, x_bf[i][:, 0:split, :], x_raw[i][:, :, 0:split])
+
+        def round_x_on_scalar(i):
+            split = VECTOR_COLS[i]
+            interleave(nc.scalar.copy, x_bf[i][:, split:CHUNK, :], x_raw[i][:, :, split:CHUNK])
 
         def quantize_x(i):
             nc.vector.quantize_mx(
@@ -121,7 +132,7 @@ def tile_rows_gglu_relu_res_kernel(tc, x, w, u, r, out):
         def apply_gates(i):
             for c in places:
                 nc.vector.scalar_tensor_tensor(
-                    out=work[i][:, SPLIT + c * CHUNK : SPLIT + (c + 1) * CHUNK],
+                    out=prod_of(SIDE * chunks[i][0] + c, cols(i).start, cols(i).stop),
                     in0=z_ps[chunks[i][1], c][:],
                     scalar=0.0,
                     in1=gate_sb[i, c][:],
@@ -129,44 +140,56 @@ def tile_rows_gglu_relu_res_kernel(tc, x, w, u, r, out):
                     op1=ALU.mult,
                 )
 
-        def add_residual(engine, i, lo, hi):
-            engine.tensor_tensor(
-                out=work[i][:, lo:hi], in0=work[i][:, SPLIT + lo : SPLIT + hi], in1=r_sb[i][:, lo:hi], op=ALU.add
-            )
+        def add_residual(engine, g, lo, hi):
+            engine.tensor_tensor(out=y[g][:, lo:hi], in0=prod_of(g, lo, hi), in1=r_sb[g][:, lo:hi], op=ALU.add)
 
-        def store(i, c):
-            nc.sync.dma_start(out=out[SIDE * chunks[i][0] + c][:, cols(i)], in_=work[i][:, c * CHUNK : (c + 1) * CHUNK])
+        def store(g, lo, hi):
+            nc.sync.dma_start(out=out[g][:, lo:hi], in_=y[g][:, lo:hi])
 
+        nc.sync.dma_start(out=x_first[:], in_=x_rows[0])
         load_weights(0)
-        for i in (0, 1, 2):
-            load_x(i)
         load_weights(1)
+        load_late_x(0)
         load_r(0)
-        load_x(3)
-        for i in (1, 2, 3):
-            load_r(i)
+        load_late_x(1)
+        for g in (1, 3, 2):
+            load_r(g)
 
-        round_weights(0)
+        round_x_on_vector(0)
+        round_x_on_scalar(0)
+        round_x_on_scalar(1)
+        round_weights(nc.vector.tensor_copy, 0)
+        quantize_x(0)
         quantize_weights(0)
-        last = len(chunks) - 1
-        for i in range(last + 3):
-            if i <= last:
-                round_x(i)
-                quantize_x(i)
-                if i == HALVES:
-                    round_weights(1)
-                    quantize_weights(1)
-                multiply(i)
-            if 0 <= i - 1 <= last:
-                copy_gates(i - 1)
-            if 0 <= i - 2 < last:
-                add_residual(nc.vector, i - 2, 0, SPLIT)
-                add_residual(nc.gpsimd, i - 2, SPLIT, SIDE * CHUNK)
-                for c in places:
-                    store(i - 2, c)
-            if i - 2 == last:
-                for c in places:
-                    add_residual(nc.vector, last, c * CHUNK, (c + 1) * CHUNK)
-                    store(last, c)
-            if 0 <= i - 1 <= last:
-                apply_gates(i - 1)
+        multiply(0)
+        round_x_on_vector(1)
+        quantize_x(1)
+        multiply(1)
+        round_weights(nc.scalar.copy, 1)
+        quantize_weights(1)
+        copy_gates(0)
+        apply_gates(0)
+
+        for g in places:
+            i = HALVES + g
+            round_x_on_vector(i)
+            round_x_on_scalar(i)
+            quantize_x(i)
+            multiply(i)
+            y[g] = sb.tile([M, N], F32, name="y_%d" % g, tag="x_bf_%d" % i, align_bytes=64)
+            add_residual(nc.gpsimd, g, 0, GPSIMD_COLS)
+            copy_gates(i - 1)
+            apply_gates(i - 1)
+            add_residual(nc.vector, g, GPSIMD_COLS, N)
+            store(g, 0, N)
+
+        add_residual(nc.vector, 3, 0, CHUNK)
+        store(3, 0, CHUNK)
+        add_residual(nc.gpsimd, 2, 0, GPSIMD_COLS)
+        store(2, 0, GPSIMD_COLS)
+        copy_gates(3)
+        apply_gates(3)
+        add_residual(nc.vector, 2, GPSIMD_COLS, N)
+        store(2, GPSIMD_COLS, N)
+        add_residual(nc.vector, 3, CHUNK, N)
+        store(3, CHUNK, N)

@@ -20,7 +20,7 @@ PAIRS = G // SIDE
 CHUNK = 512
 HALVES = N // CHUNK
 RUN = 2
-VECTOR_COLS = (256, 256, 256, 320)
+VECTOR_COLS = (320, 320, 384, 256)
 GPSIMD_COLS = 384
 
 
@@ -46,21 +46,19 @@ def tile_rows_gglu_relu_res_kernel(tc, x, w, u, r, out):
         chunks = [(s, h) for s in range(PAIRS) for h in range(HALVES)]
         steps = range(len(chunks))
         places = range(SIDE)
-        x_first = sb.tile([P, PACK, N], F32)
-        x_late = [sb.tile([P, PACK, CHUNK], F32, name="x_late_%d" % h) for h in range(HALVES)]
-        x_raw = [x_first[:, :, 0:CHUNK], x_first[:, :, CHUNK:N], x_late[0][:], x_late[1][:]]
-        x_bf = [sb.tile([P, CHUNK, PACK], BF16, name="x_bf_%d" % i, tag="x_bf_%d" % i, align_bytes=64) for i in steps]
+        x_raw = [sb.tile([P, PACK, CHUNK], F32, name="x_raw_%d" % i) for i in steps]
+        x_bf = [sb.tile([P, CHUNK, PACK], BF16, name="x_bf_%d" % i, align_bytes=64) for i in steps]
         x_codes = [sb.tile([P, CHUNK], U32, name="x_codes_%d" % i, align_bytes=64) for i in steps]
         x_scales = [sb.tile([P, CHUNK], U8, name="x_scales_%d" % i, align_bytes=64) for i in steps]
         w_raw = [sb.tile([P, PACK, M], F32, name="w_raw_%d" % s) for s in range(PAIRS)]
         u_raw = [sb.tile([P, PACK, M], F32, name="u_raw_%d" % s) for s in range(PAIRS)]
-        wu_bf = [sb.tile([P, 2 * M, PACK], BF16, name="wu_bf_%d" % s, align_bytes=64) for s in range(PAIRS)]
+        wu_bf = [sb.tile([P, 2 * M, PACK], BF16, name="wu_bf_%d" % s, tag="wu_bf_%d" % s, align_bytes=64) for s in range(PAIRS)]
         wu_codes = [sb.tile([P, 2 * M], U32, name="wu_codes_%d" % s, align_bytes=64) for s in range(PAIRS)]
         wu_scales = [sb.tile([P, 2 * M], U8, name="wu_scales_%d" % s, align_bytes=64) for s in range(PAIRS)]
         r_sb = [sb.tile([M, N], F32, name="r_sb_%d" % g) for g in range(G)]
         gate_sb = {(i, c): sb.tile([M, CHUNK], F32, name="gate_sb_%d_%d" % (i, c)) for i in steps for c in places}
         prod = [sb.tile([M, N], F32, name="prod_%d" % g) for g in range(G)]
-        y = {g: sb.tile([M, N], F32, name="y_%d" % g) for g in (2, 3)}
+        y = {g: sb.tile([M, N], F32, name="y_%d" % g) for g in (1, 2, 3)}
 
         def prod_of(g, lo, hi):
             if g == 3 and hi <= CHUNK:
@@ -78,8 +76,8 @@ def tile_rows_gglu_relu_res_kernel(tc, x, w, u, r, out):
             nc.sync.dma_start(out=w_raw[s][:], in_=w_rows[s])
             nc.sync.dma_start(out=u_raw[s][:], in_=u_rows[s])
 
-        def load_late_x(h):
-            nc.sync.dma_start(out=x_late[h][:], in_=x_rows[1][:, :, cols(h)])
+        def load_x(i):
+            nc.sync.dma_start(out=x_raw[i][:], in_=x_rows[chunks[i][0]][:, :, cols(i)])
 
         def load_r(g):
             nc.sync.dma_start(out=r_sb[g][:], in_=r[g])
@@ -129,8 +127,8 @@ def tile_rows_gglu_relu_res_kernel(tc, x, w, u, r, out):
             for c in places:
                 nc.scalar.copy(out=gate_sb[i, c][:], in_=gate_ps[chunks[i][1], c][:])
 
-        def apply_gates(i):
-            for c in places:
+        def apply_gates(i, which=places):
+            for c in which:
                 nc.vector.scalar_tensor_tensor(
                     out=prod_of(SIDE * chunks[i][0] + c, cols(i).start, cols(i).stop),
                     in0=z_ps[chunks[i][1], c][:],
@@ -146,42 +144,42 @@ def tile_rows_gglu_relu_res_kernel(tc, x, w, u, r, out):
         def store(g, lo, hi):
             nc.sync.dma_start(out=out[g][:, lo:hi], in_=y[g][:, lo:hi])
 
-        nc.sync.dma_start(out=x_first[:], in_=x_rows[0])
         load_weights(0)
+        for i in (0, 1, 2):
+            load_x(i)
         load_weights(1)
-        load_late_x(0)
         load_r(0)
-        load_late_x(1)
+        load_x(3)
         for g in (1, 3, 2):
             load_r(g)
 
-        round_x_on_vector(0)
-        round_x_on_scalar(0)
-        round_x_on_scalar(1)
-        round_weights(nc.vector.tensor_copy, 0)
-        quantize_x(0)
+        round_weights(nc.scalar.copy, 0)
         quantize_weights(0)
-        multiply(0)
-        round_x_on_vector(1)
-        quantize_x(1)
-        multiply(1)
-        round_weights(nc.scalar.copy, 1)
-        quantize_weights(1)
-        copy_gates(0)
-        apply_gates(0)
-
-        for g in places:
-            i = HALVES + g
+        for i in (0, 1, 2):
             round_x_on_vector(i)
             round_x_on_scalar(i)
             quantize_x(i)
+            if i == HALVES:
+                round_weights(nc.scalar.copy, 1)
+                quantize_weights(1)
+                y[0] = sb.tile([M, N], F32, name="y_0", tag="wu_bf_1", align_bytes=64)
+                add_residual(nc.gpsimd, 0, 0, GPSIMD_COLS)
             multiply(i)
-            y[g] = sb.tile([M, N], F32, name="y_%d" % g, tag="x_bf_%d" % i, align_bytes=64)
-            add_residual(nc.gpsimd, g, 0, GPSIMD_COLS)
-            copy_gates(i - 1)
-            apply_gates(i - 1)
-            add_residual(nc.vector, g, GPSIMD_COLS, N)
-            store(g, 0, N)
+            if i > 0:
+                copy_gates(i - 1)
+                apply_gates(i - 1)
+        add_residual(nc.vector, 0, GPSIMD_COLS, N)
+        store(0, 0, N)
+
+        copy_gates(2)
+        apply_gates(2, (0,))
+        round_x_on_vector(3)
+        round_x_on_scalar(3)
+        apply_gates(2, (1,))
+        quantize_x(3)
+        multiply(3)
+        add_residual(nc.vector, 1, 0, N)
+        store(1, 0, N)
 
         add_residual(nc.vector, 3, 0, CHUNK)
         store(3, 0, CHUNK)

from contextlib import ExitStack

import concourse.mybir as mybir

G, D, M, N = 4, 256, 128, 1024
FLOPS = 2 * 2 * G * D * M * N

F32 = mybir.dt.float32
BF16 = mybir.dt.bfloat16
U32 = mybir.dt.uint32
U8 = mybir.dt.uint8
FP8X4 = mybir.dt.float8_e4m3fn_x4
ALU = mybir.AluOpType

P = 128
PACK = 4
ROWS = D // PACK
SIDE = P // ROWS
PAIRS = G // SIDE
CHUNK = 512
HALVES = N // CHUNK
RUN = 2
VECTOR_COLS = (320, 320, 384, 256)
GPSIMD_COLS = 384


def interleave(copy, dst, src):
    copy(
        out=dst.rearrange("p (c i) j -> p c j i", i=RUN),
        in_=src.rearrange("p j (c i) -> p c j i", i=RUN),
    )


def tile_rows_gglu_relu_res_kernel(tc, x, w, u, r, out):
    nc = tc.nc
    x_rows = x.rearrange("(s c) (p j) n -> s (c p) j n", c=SIDE, j=PACK)
    w_rows = w.rearrange("(s c) (p j) m -> s (c p) j m", c=SIDE, j=PACK)
    u_rows = u.rearrange("(s c) (p j) m -> s (c p) j m", c=SIDE, j=PACK)


    with ExitStack() as ctx:
        sb = ctx.enter_context(tc.tile_pool(name="sb", bufs=1))
        psum = ctx.enter_context(tc.psum_pool(name="psum", bufs=1))
        ctx.enter_context(tc.manual_schedule())

        chunks = [(s, h) for s in range(PAIRS) for h in range(HALVES)]
        steps = range(len(chunks))
        places = range(SIDE)
        x_raw = [sb.tile([P, PACK, CHUNK], F32, name="x_raw_%d" % i) for i in steps]
        x_bf = [sb.tile([P, CHUNK, PACK], BF16, name="x_bf_%d" % i, align_bytes=64) for i in steps]
        x_codes = [sb.tile([P, CHUNK], U32, name="x_codes_%d" % i, align_bytes=64) for i in steps]
        x_scales = [sb.tile([P, CHUNK], U8, name="x_scales_%d" % i, align_bytes=64) for i in steps]
        w_raw = [sb.tile([P, PACK, M], F32, name="w_raw_%d" % s) for s in range(PAIRS)]
        u_raw = [sb.tile([P, PACK, M], F32, name="u_raw_%d" % s) for s in range(PAIRS)]
        wu_bf = [sb.tile([P, 2 * M, PACK], BF16, name="wu_bf_%d" % s, tag="wu_bf_%d" % s, align_bytes=64) for s in range(PAIRS)]
        wu_codes = [sb.tile([P, 2 * M], U32, name="wu_codes_%d" % s, align_bytes=64) for s in range(PAIRS)]
        wu_scales = [sb.tile([P, 2 * M], U8, name="wu_scales_%d" % s, align_bytes=64) for s in range(PAIRS)]
        r_sb = [sb.tile([M, N], F32, name="r_sb_%d" % g) for g in range(G)]
        gate_sb = {(i, c): sb.tile([M, CHUNK], F32, name="gate_sb_%d_%d" % (i, c)) for i in steps for c in places}
        prod = [sb.tile([M, N], F32, name="prod_%d" % g) for g in range(G)]
        y = {g: sb.tile([M, N], F32, name="y_%d" % g) for g in (1, 2, 3)}

        def prod_of(g, lo, hi):
            if g == 3 and hi <= CHUNK:
                return y[2][:, lo:hi]
            return prod[g][:, lo:hi]

        z_ps = {(h, c): psum.tile([M, CHUNK], F32, name="z_ps_%d_%d" % (h, c)) for h in range(HALVES) for c in places}
        gate_ps = {(h, c): psum.tile([M, CHUNK], F32, name="gate_ps_%d_%d" % (h, c)) for h in range(HALVES) for c in places}

        def cols(i):
            h = chunks[i][1]
            return slice(h * CHUNK, (h + 1) * CHUNK)

        def load_weights(s):
            nc.sync.dma_start(out=w_raw[s][:], in_=w_rows[s])
            nc.sync.dma_start(out=u_raw[s][:], in_=u_rows[s])

        def load_x(i):
            nc.sync.dma_start(out=x_raw[i][:], in_=x_rows[chunks[i][0]][:, :, cols(i)])

        def load_r(g):
            nc.sync.dma_start(out=r_sb[g][:], in_=r[g])

        def round_weights(copy, s):
            interleave(copy, wu_bf[s][:, 0:M, :], w_raw[s][:])
            interleave(copy, wu_bf[s][:, M : 2 * M, :], u_raw[s][:])

        def quantize_weights(s):
            nc.vector.quantize_mx(
                out=wu_codes[s][:].bitcast(FP8X4),
                scales=wu_scales[s][:],
                in_=wu_bf[s][:].rearrange("p m j -> p (m j)"),
            )

        def round_x_on_vector(i):
            split = VECTOR_COLS[i]
            interleave(nc.vector.tensor_copy, x_bf[i][:, 0:split, :], x_raw[i][:, :, 0:split])

        def round_x_on_scalar(i):
            split = VECTOR_COLS[i]
            interleave(nc.scalar.copy, x_bf[i][:, split:CHUNK, :], x_raw[i][:, :, split:CHUNK])

        def quantize_x(i):
            nc.vector.quantize_mx(
                out=x_codes[i][:].bitcast(FP8X4),
                scales=x_scales[i][:],
                in_=x_bf[i][:].rearrange("p n j -> p (n j)"),
            )

        def multiply(i):
            s, h = chunks[i]
            for banks, m_cols in ((gate_ps, slice(M, 2 * M)), (z_ps, slice(0, M))):
                for c in places:
                    rows = slice(c * ROWS, (c + 1) * ROWS)
                    nc.tensor.matmul_mx(
                        out=banks[h, c][:],
                        lhsT=wu_codes[s][rows, m_cols].bitcast(FP8X4),
                        lhsT_scale=wu_scales[s][rows, m_cols],
                        rhs=x_codes[i][rows, :].bitcast(FP8X4),
                        rhs_scale=x_scales[i][rows, :],
                        start=True,
                        stop=True,
                    )

        def copy_gates(i):
            for c in places:
                nc.scalar.copy(out=gate_sb[i, c][:], in_=gate_ps[chunks[i][1], c][:])

        def apply_gates(i, which=places):
            for c in which:
                nc.vector.scalar_tensor_tensor(
                    out=prod_of(SIDE * chunks[i][0] + c, cols(i).start, cols(i).stop),
                    in0=z_ps[chunks[i][1], c][:],
                    scalar=0.0,
                    in1=gate_sb[i, c][:],
                    op0=ALU.max,
                    op1=ALU.mult,
                )

        def add_residual(engine, g, lo, hi):
            engine.tensor_tensor(out=y[g][:, lo:hi], in0=prod_of(g, lo, hi), in1=r_sb[g][:, lo:hi], op=ALU.add)

        def store(g, lo, hi):
            nc.sync.dma_start(out=out[g][:, lo:hi], in_=y[g][:, lo:hi])

        load_weights(0)
        for i in (0, 1, 2):
            load_x(i)
        load_weights(1)
        load_r(0)
        load_x(3)
        for g in (1, 3, 2):
            load_r(g)

        round_weights(nc.scalar.copy, 0)
        quantize_weights(0)
        for i in (0, 1, 2):
            round_x_on_vector(i)
            round_x_on_scalar(i)
            quantize_x(i)
            if i == HALVES:
                round_weights(nc.scalar.copy, 1)
                quantize_weights(1)
                y[0] = sb.tile([M, N], F32, name="y_0", tag="wu_bf_1", align_bytes=64)
                add_residual(nc.gpsimd, 0, 0, GPSIMD_COLS)
            multiply(i)
            if i > 0:
                copy_gates(i - 1)
                apply_gates(i - 1)
        add_residual(nc.vector, 0, GPSIMD_COLS, N)
        store(0, 0, N)

        copy_gates(2)
        apply_gates(2, (0,))
        round_x_on_vector(3)
        round_x_on_scalar(3)
        apply_gates(2, (1,))
        quantize_x(3)
        multiply(3)
        add_residual(nc.vector, 1, 0, N)
        store(1, 0, N)

        add_residual(nc.vector, 3, 0, CHUNK)
        store(3, 0, CHUNK)
        add_residual(nc.gpsimd, 2, 0, GPSIMD_COLS)
        store(2, 0, GPSIMD_COLS)
        copy_gates(3)
        apply_gates(3)
        add_residual(nc.vector, 2, GPSIMD_COLS, N)
        store(2, GPSIMD_COLS, N)
        add_residual(nc.vector, 3, CHUNK, N)
        store(3, CHUNK, N)
